import numpy as np, ml_dtypes
CORES = [36,164,52,180,100,228,116,244]
N = 8
import mx_ref
BF = ml_dtypes.bfloat16
def entries(a):
    return np.ascontiguousarray(a.T).reshape(-1)
def table(e):
    return np.ascontiguousarray(np.reshape(e, (-1, 16)).T).astype(np.int32)
def gentries(a):
    return np.ascontiguousarray(a.reshape(8, 16, -1).transpose(0, 2, 1)).reshape(8, -1)
def gtable(e):
    e = np.asarray(e); return np.ascontiguousarray(e.reshape(8, -1, 16).transpose(0, 2, 1)).reshape(128, -1).astype(np.int32)
def tile(rs):
    return np.stack(rs, axis=2).reshape(128, -1).astype(BF)
def cut(t, i, w=512):
    return t[:, w * i:w * i + w]
def f(rng, *shape):
    return mx_ref.flush((rng.standard_normal(shape, dtype=np.float32) * np.exp2(rng.integers(-2, 3, shape[:-1] + (1,)))).astype(BF))
def wide(rng, *shape, cols=0):
    v = rng.standard_normal(shape, dtype=np.float32) * np.exp2(rng.integers(-12, 13, shape)).astype(np.float32)
    if cols: v *= np.repeat(np.exp2(rng.integers(-cols, cols + 1, shape[:-2] + (1, shape[-1] // 4))) * (rng.random(shape[:-2] + (1, shape[-1] // 4)) > 0.0625), 4, axis=-1).astype(np.float32)
    return mx_ref.flush(v.astype(BF))
T, CAPP, P = 256, 48, 256
SL = N * CAPP
G = 8
def pieces(rng, how):
    if how == "ones": n = np.ones((G, SL), int)
    elif how == "full":
        n = T - rng.integers(0, 8, (G, SL)); n[:, ::4] = T
    elif how == "powers":
        k = [1 << i for i in range(T.bit_length())]; k = sorted(set(k + [i + 1 for i in k if i < T]))
        n = rng.permuted(np.tile(np.resize(k, SL), (G, 1)), axis=1)
    else: n = np.where(rng.random((G, SL)) < 0.5, rng.integers(1, T + 1, (G, SL)), np.clip(np.exp2(rng.uniform(0, T.bit_length() - 1, (G, SL))).astype(int), 1, T))
    s = rng.integers(0, T - n + 1)
    if how == "full": s[:] = 0
    if how == "nested":
        for g in range(G):
            for r in range(N):
                m = rng.integers(0, T)
                b = np.sort(rng.choice(rng.integers(0, m + 1, 16), CAPP)); e = np.sort(rng.choice(rng.integers(m, T, 16), CAPP))[::-1]
                k = r * CAPP + rng.permutation(CAPP); s[g, k] = b; n[g, k] = e - b + 1
    return s, n
def lists(rng, how="any", every=False):
    held = np.zeros((N, N, CAPP), bool)
    for r in range(N):
        n = rng.integers(0, CAPP + 1, N); n[(r + rng.integers(1, N)) % N] = CAPP
        for q in range(N): held[q, r, rng.permutation(CAPP)[:CAPP if every else n[q]]] = True
    d = {"lo": [], "ln": [], "pf": [], "pg": []}
    for q in range(N):
        s, n = pieces(rng, how); e = ~held[q].reshape(-1)
        s[:, e] = -1; n[:, e] = 0
        d["lo"].append(gtable(s)); d["ln"].append(gtable(n))
    who = rng.permutation(N)
    for r in range(N):
        k = rng.permutation(np.flatnonzero(held[:, r]))
        first = rng.permutation(np.resize(k, P))
        second = np.where(rng.random(P) < 0.25, -1, rng.choice(k, P))
        if how == "ones":
            if r == who[0]:
                first[rng.permutation(P)[:P // 2]] = k[0]; second[rng.permutation(P)[:P // 2]] = k[0]
            if r == who[1]: second[:] = -1
            if r == who[2]: second = rng.choice(k, P)
        d["pf"].append(table(first))
        d["pg"].append(table(second))
    return {k: np.stack(t) for k, t in d.items()}
def setup_inputs(rng):
    return {"x": f(rng, N, 128, 4 * T), "a": f(rng, N, 128, 2048), "u": f(rng, N, 128, 512), "v": f(rng, N, 128, 512), **lists(rng)}
def setup_inputs_ones(rng):
    return {**setup_inputs(rng), **lists(rng, "ones")}
def setup_inputs_full(rng):
    return {**setup_inputs(rng), **lists(rng, "full", True)}
def setup_inputs_powers(rng):
    return {**setup_inputs(rng), **lists(rng, "powers", True)}
def setup_inputs_nested(rng):
    return {**setup_inputs(rng), **lists(rng, "nested", True)}
def setup_inputs_spread(rng):
    d = setup_inputs(rng); d["x"] = wide(rng, N, 128, 4 * T, cols=8); return d
def check_inputs(d):
    b = []; held = []
    for q in range(N):
        s, n = gentries(d["lo"][q]).reshape(G, -1), gentries(d["ln"][q]).reshape(G, -1)
        e = s == -1; held.append(~e[0])
        if s.min() < -1 or s.max() >= T or (e != e[:1]).any(): b.append("lo")
        if (n[e] != 0).any() or (n[~e] < 1).any() or (n[~e] > T - s[~e]).any(): b.append("ln")
    for r in range(N):
        h = np.concatenate([held[q][r * CAPP:r * CAPP + CAPP] for q in range(N)])
        for k, least in (("pf", 0), ("pg", -1)):
            j = entries(d[k][r])
            if j.min() < least or j.max() >= SL or not h[j[(j >= 0) & (j < SL)]].all(): b.append(k)
    return b
def reference(x, a, u, v, lo, ln, pf, pg):
    sent = []
    for q in range(N):
        X = mx_ref.quantize(x[q])
        Z = np.stack([mx_ref.matmul(mx_ref.quantize(np.ascontiguousarray(cut(a[q], i))), X) for i in range(4)])
        h = np.maximum(Z, np.float32(0)) * np.float32(0.05)
        s, n = gentries(lo[q]), gentries(ln[q])
        R = np.zeros((4, 128, SL), np.float32)
        for k in range(SL):
            for g in range(8):
                if n[g, k]: R[:, 16 * g:16 * g + 16, k] = h[:, 16 * g:16 * g + 16, s[g, k]:s[g, k] + n[g, k]].max(axis=2)
        sent.append([mx_ref.quantize(np.ascontiguousarray(tile([R[i][:, CAPP * r:CAPP * r + CAPP] for i in range(4)]))) for r in range(N)])
    y = np.zeros((N, 128, P), np.float32)
    for r in range(N):
        V, U = mx_ref.quantize(v[r]), mx_ref.quantize(u[r])
        zv = np.concatenate([mx_ref.matmul(V, sent[q][r]) for q in range(N)], axis=1)
        zu = np.concatenate([mx_ref.matmul(U, sent[q][r]) for q in range(N)], axis=1)
        first, second = entries(pf[r]), entries(pg[r])
        y[r] = zv[:, first]
        two = second >= 0
        y[r][:, two] += zu[:, second[two]]
    return {"y": y}

@@ -1,0 +1,309 @@
+from concourse.bass import DstId, RemoteDMATransfer
+from concourse.mybir import dt, AluOpType, ActivationFunctionType
+
+N, CAPP, COLS, P = 8, 48, 256, 256
+SL = N * CAPP
+LW = SL // 16
+LAND = (N - 1) * CAPP
+LEV = 7
+BY_S, BY_G = (1, 2), (3,)
+PACKED = BY_S + BY_G
+ZW = 392
+
+
+def width(k):
+    return COLS // 2 if k in PACKED else COLS - (1 << k)
+
+
+def layout():
+    b, f, m, at, am = {}, {}, {}, 2 + COLS, 0
+    for k in range(1, LEV + 1):
+        b[k], f[k], m[k] = at, at + width(k), am
+        at, am = at + 2 * width(k), am + width(k)
+    return b, f, m, at, am
+
+
+BK, FK, MK, TW, MW = layout()
+TS = (TW + 15) // 16 * 16
+
+SCRATCH = {
+    "lol": ("sbuf", [128, 2 * LW], "int32"),
+    "lr": ("sbuf", [128, 2 * LW], "float32"),
+    "tj": ("sbuf", [128, 16 * LW], "bfloat16"),
+    "dif": ("sbuf", [128, 8 * LW], "float32"),
+    "cb": ("sbuf", [128, 8 * LW], "float32"),
+    "cf": ("sbuf", [128, 8 * LW], "float32"),
+    "pb": ("sbuf", [128, 8 * LW], "float32"),
+    "pq": ("sbuf", [128, 8 * LW], "float32"),
+    "offl": ("sbuf", [128, LW], "uint16"),
+    "offr": ("sbuf", [128, LW], "uint16"),
+    "xt": ("sbuf", [128, 1024], "bfloat16"),
+    "at": ("sbuf", [128, 2048], "bfloat16"),
+    "uvt": ("sbuf", [128, 1024], "bfloat16"),
+    "qx": ("sbuf", [128, 256], "float8_e4m3fn_x4"),
+    "sx": ("sbuf", [128, 256], "uint8"),
+    "qa": ("sbuf", [128, 512], "float8_e4m3fn_x4"),
+    "sa": ("sbuf", [128, 512], "uint8"),
+    "quv": ("sbuf", [128, 256], "float8_e4m3fn_x4"),
+    "suv": ("sbuf", [128, 256], "uint8"),
+    "h0": ("sbuf", [128, 4, 4, 4, 4], "bfloat16"),
+    "h1": ("sbuf", [128, 4, 4, 4, 4], "bfloat16"),
+    "h2": ("sbuf", [128, 4, 4, 4, 4], "bfloat16"),
+    "h3": ("sbuf", [128, 4, 4, 4, 4], "bfloat16"),
+    "tab": ("sbuf", [128, 4 * TS], "bfloat16"),
+    "mask": ("sbuf", [128, MW], "bfloat16"),
+    "pk": ("sbuf", [128, 4 * len(PACKED) * COLS], "bfloat16"),
+    "left": ("sbuf", [128, 4 * SL], "bfloat16"),
+    "pt": ("sbuf", [128, 4 * SL], "bfloat16"),
+    "qp": ("sbuf", [128, SL], "float8_e4m3fn_x4"),
+    "sp": ("sbuf", [128, SL], "uint8"),
+    "lc": ("sbuf", [128, LAND], "float8_e4m3fn_x4"),
+    "ls": ("sbuf", [128, LAND], "uint8"),
+    "lp": ("sbuf", [128, 32], "int32"),
+    "offp": ("sbuf", [128, 32], "uint16"),
+    "zv": ("sbuf", [128, ZW], "float32"),
+    "zu": ("sbuf", [128, ZW], "float32"),
+    "first": ("sbuf", [128, P], "float32"),
+    "yt": ("sbuf", [128, P], "float32"),
+    "ps": ("psum", [128, 4096], "float32"),
+}
+SEMAPHORES = ["vs", "ss", "ts", "gs", "lst", "lx", "la0", "la1", "la2", "la3", "luv", "lpl", "arr", "sent", "st0", "st1"]
+
+
+def half(h, k, bit):
+    ix = [slice(None)] * 5
+    ix[4 - k // 2] = slice(2 * bit, 2 * bit + 2) if k % 2 else slice(bit, None, 2)
+    return h[tuple(ix)]
+
+
+def falling(buf, a, w):
+    return buf[:, a + w - 1:(a - 1 if a else None):-1]
+
+
+def rank_program(g, core, T, topo):
+    rank = T.rank_of(core)
+    if rank is None:
+        return
+    V, S, PE, Y = g.vector, g.scalar, g.tensor, g.sync
+    A, F = AluOpType, ActivationFunctionType
+    vs, ss, ts, gs = T.sem.vs, T.sem.ss, T.sem.ts, T.sem.gs
+    n = {"v": 0, "s": 0, "t": 0, "g": 0}
+
+    def v(i):
+        n["v"] += 1
+        i.then_inc(vs, 1)
+        return n["v"]
+
+    def s(i):
+        n["s"] += 1
+        i.then_inc(ss, 1)
+        return n["s"]
+
+    def t(i):
+        n["t"] += 1
+        i.then_inc(ts, 1)
+        return n["t"]
+
+    def gp(i):
+        n["g"] += 1
+        i.then_inc(gs, 1)
+        return n["g"]
+
+    def bank(b, w):
+        return T.ps[:, 512 * b:512 * b + w]
+
+    S.dma_start(T.lol[:, 0:LW], T.lo[:]).then_inc(T.sem.lst, 16)
+    S.dma_start(T.lol[:, LW:2 * LW], T.ln[:]).then_inc(T.sem.lst, 16)
+    Y.dma_start(T.xt[:], T.x[:]).then_inc(T.sem.lx, 16)
+    for i in range(4):
+        Y.dma_start(T["at"][:, 512 * i:512 * i + 512], T.a[:, 512 * i:512 * i + 512]).then_inc(T.sem["la%d" % i], 16)
+    Y.dma_start(T.uvt[:, 0:512], T.u[:]).then_inc(T.sem.luv, 16)
+    Y.dma_start(T.uvt[:, 512:1024], T.v[:]).then_inc(T.sem.luv, 16)
+    for k in range(8):
+        Y.dma_start(T.lp[16 * k:16 * k + 16, 0:16], T.pf[:]).then_inc(T.sem.lpl, 16)
+        Y.dma_start(T.lp[16 * k:16 * k + 16, 16:32], T.pg[:]).then_inc(T.sem.lpl, 16)
+
+    ones = v(V.memset(T.mask[:], 1.0))
+    v(V.memset(T.tj[:, 0::8], 0.0))
+    v(V.memset(T.cb[:, 7::8], 0.0))
+    v(V.memset(T.cf[:, 7::8], 0.0))
+    v(V.memset(T.tab[:, 0::TS], 0.0))
+    v(V.memset(T.tab[:, 1 + COLS::TS], 0.0))
+    for k in range(1, LEV + 1):
+        if k not in PACKED:
+            v(V.memset(T.cb[:, 7 - k::8], BK[k] - 1.0))
+            v(V.memset(T.cf[:, 7 - k::8], FK[k] - (1 << k) - 1.0))
+
+    V.wait_ge(T.sem.lst, 32)
+    v(V.tensor_scalar(T.lr[:, 0:LW], T.lol[:, 0:LW], 1, None, A.add))
+    lists = v(V.tensor_tensor(T.lr[:, LW:2 * LW], T.lol[:, 0:LW], T.lol[:, LW:2 * LW], A.add))
+    V.wait_ge(vs, ones)
+    for k in range(1, LEV + 1):
+        consts = v(V.memset(T.mask[:, MK[k]:MK[k] + width(k):1 << k], 0.0))
+
+    S.wait_ge(vs, lists)
+    for j in range(LEV, 0, -1):
+        floors = s(S.activation(T.tj[:, 8 - j::8], T.lr[:], F.Identity, bias=128.5 - 2.0 ** -(j + 1), scale=2.0 ** -j))
+    S.wait_ge(ss, floors)
+    for j in PACKED:
+        w = 2.0 ** (j - 1)
+        s(S.activation(T.cb[:, 7 - j::8], T.tj[:, 8 * LW + 8 - j::8], F.Identity, bias=BK[j] - 1 + w + 129 * w, scale=-w))
+        cands = s(S.activation(T.cf[:, 7 - j::8], T.tj[:, 8 * LW + 8 - j::8], F.Identity, bias=FK[j] - 1 - w + 129 * w, scale=-w))
+
+    def offsets():
+        V.wait_ge(ss, floors)
+        d = v(V.tensor_tensor(T.dif[:], T.tj[:, 8 * LW:16 * LW], T.tj[:, 0:8 * LW], A.is_gt))
+        V.wait_ge(ss, cands)
+        V.wait_ge(vs, d)
+        b = v(V.tensor_tensor_scan(T.pb[:], T.dif[:], T.cb[:], 0.0, A.mult, A.max))
+        f = v(V.tensor_tensor_scan(T.pq[:], T.dif[:], T.cf[:], 0.0, A.mult, A.max))
+        V.wait_ge(vs, b)
+        v(V.tensor_tensor(T.offl[:], T.pb[:, 7::8], T.lr[:, 0:LW], A.add))
+        V.wait_ge(vs, f)
+        return v(V.tensor_tensor(T.offr[:], T.pq[:, 7::8], T.lr[:, LW:2 * LW], A.add))
+
+    def product_a(i):
+        V.wait_ge(T.sem["la%d" % i], 16)
+        c = slice(128 * i, 128 * i + 128)
+        q = v(V.quantize_mx(T.qa[:, c], T.sa[:, c], T["at"][:, 512 * i:512 * i + 512]))
+        PE.wait_ge(vs, q)
+        return t(PE.matmul_mx(bank(i, COLS), T.qa[:, c], T.sa[:, c], T.qx[:], T.sx[:], True, True))
+
+    def packed(i, k, bit):
+        return COLS * (len(PACKED) * i + PACKED.index(k)) + 128 * bit
+
+    def result(i, z):
+        S.wait_ge(ts, z)
+        r = s(S.activation(T.tab[:, TS * i + 1:TS * i + 1 + COLS], bank(i, COLS), F.Relu, scale=0.05))
+        h = T["h%d" % i]
+        c = s(S.activation(h[:], bank(i, COLS), F.Relu, scale=0.05))
+        S.wait_ge(ss, c)
+        g.wait_ge(ss, c)
+        ready = {}
+        for k in PACKED:
+            for bit in (0, 1):
+                a = packed(i, k, bit)
+                if k in BY_S:
+                    ready[k] = (ss, s(S.activation(T.pk[:, a:a + 128], half(h, k, bit), F.Copy)))
+                else:
+                    ready[k] = (gs, gp(g.affine_select(T.pk[:, a:a + 128], half(h, k, bit), [[0, 128]], A.is_equal, 0.0, 0, 0)))
+        return r, ready
+
+    def tables(i, r):
+        h, ready = r
+        V.wait_ge(ss, h)
+        V.wait_ge(vs, consts)
+        for k in range(LEV, 0, -1):
+            w, h0 = width(k), TS * i + 1
+            m = T.mask[:, MK[k]:MK[k] + w]
+            if k in PACKED:
+                V.wait_ge(*ready[k])
+                fall = falling(T.pk, packed(i, k, 0), 128)
+                rise = T.pk[:, packed(i, k, 1):packed(i, k, 1) + 128]
+            else:
+                fall, rise = falling(T.tab, h0, w), T.tab[:, h0 + COLS - w:h0 + COLS]
+            v(V.tensor_tensor_scan(falling(T.tab, TS * i + BK[k], w), m, fall, 0.0, A.mult, A.max))
+            last = v(V.tensor_tensor_scan(T.tab[:, TS * i + FK[k]:TS * i + FK[k] + w], m, rise, 0.0, A.mult, A.max))
+        return last
+
+    def left(i, w):
+        S.wait_ge(vs, w)
+        return s(S.activation(T.left[:, SL * i:SL * i + SL], T.tab[:, TS * i:TS * i + TW].indirect(T.offl[:, 0:LW]), F.Copy))
+
+    def right(i, w):
+        V.wait_ge(ss, w)
+        return v(V.tensor_tensor(T.pt[:, i:4 * SL:4], T.tab[:, TS * i:TS * i + TW].indirect(T.offr[:, 0:LW]), T.left[:, SL * i:SL * i + SL], A.max))
+
+    V.wait_ge(T.sem.lx, 16)
+    v(V.quantize_mx(T.qx[:], T.sx[:], T.xt[:]))
+    z0 = product_a(0)
+    offs = offsets()
+    z1 = product_a(1)
+    r0 = result(0, z0)
+    r1 = result(1, z1)
+    V.wait_ge(vs, offs)
+    w0 = tables(0, r0)
+    r2 = result(2, product_a(2))
+    l0 = left(0, w0)
+    w1 = tables(1, r1)
+    r3 = result(3, product_a(3))
+    l1 = left(1, w1)
+    w2 = tables(2, r2)
+    l2 = left(2, w2)
+    right(0, l0)
+    w3 = tables(3, r3)
+    l3 = left(3, w3)
+    right(1, l1)
+    right(2, l2)
+    full = right(3, l3)
+    V.wait_ge(vs, full)
+    pieces = v(V.quantize_mx(T.qp[:], T.sp[:], T.pt[:]))
+
+    g.wait_ge(vs, pieces)
+    for src, dst, codes in (("qp", "lc", True), ("sp", "ls", False)):
+        tr = []
+        for i, r in enumerate([r for r in range(N) if r != rank]):
+            d = T.cores[r]
+            rid, pid = topo.addr(d, core)
+            at = CAPP * (rank if rank < r else rank - 1)
+            a, b = T[src][:, CAPP * r:CAPP * r + CAPP], T[dst][:, at:at + CAPP]
+            if codes:
+                a, b = a.bitcast(dt.uint8), b.bitcast(dt.uint8)
+            tr.append(RemoteDMATransfer(dst_ids=[DstId(rid=rid, pnc=pid)], dma_engine_mask=1 << topo.engines(core, d)[i],
+                                        remote_sem=T.sem.arr, src=a, dst=b))
+        g.remote_dma_fused(tr, local_sem=T.sem.sent)
+
+    V.wait_ge(T.sem.luv, 32)
+    quv = v(V.quantize_mx(T.quv[:], T.suv[:], T.uvt[:]))
+    v(V.memset(T.zv[:, 0:1], 0.0))
+    v(V.memset(T.zu[:, 0:1], 0.0))
+    V.wait_ge(T.sem.lpl, 256)
+    places = v(V.tensor_scalar(T.offp[:], T.lp[:], 1, None, A.add))
+
+    def product(b, w, c0, codes, scales, a0):
+        return t(PE.matmul_mx(bank(b, w), T.quv[:, c0:c0 + 128], T.suv[:, c0:c0 + 128], codes[:, a0:a0 + w], scales[:, a0:a0 + w], True, True))
+
+    def copy_v(b, z, w, a, to):
+        S.wait_ge(ts, z)
+        return s(S.activation(T.zv[:, to:to + w], T.ps[:, 512 * b + a:512 * b + a + w], F.Copy))
+
+    def copy_u(b, z, w, a, to):
+        V.wait_ge(ts, z)
+        return v(V.tensor_copy(T.zu[:, to:to + w], T.ps[:, 512 * b + a:512 * b + a + w]))
+
+    own = min(CAPP * rank, SL - 128)
+    PE.wait_ge(vs, quv)
+    PE.wait_ge(ss, l3)
+    z = product(4, 128, 128, T.qp, T.sp, own)
+    copy_v(4, z, CAPP, CAPP * rank - own, 1 + CAPP * rank)
+    z = product(5, 128, 0, T.qp, T.sp, own)
+    copy_u(5, z, CAPP, CAPP * rank - own, 1 + CAPP * rank)
+
+    mine = CAPP * rank
+    cut = mine if 128 <= mine <= LAND - 128 else LAND // 2
+    PE.wait_ge(T.sem.arr, 2 * (N - 1))
+    for a, b, bv, bu in ((0, cut, 6, 7), (cut, LAND, 0, 1)):
+        parts = [(lo, hi) for lo, hi in ((a, min(b, mine)), (max(a, mine), b)) if lo < hi]
+        z = product(bv, b - a, 128, T.lc, T.ls, a)
+        for lo, hi in parts:
+            cv = copy_v(bv, z, hi - lo, lo - a, 1 + lo + (CAPP if lo >= mine else 0))
+        z = product(bu, b - a, 0, T.lc, T.ls, a)
+        for lo, hi in parts:
+            cu = copy_u(bu, z, hi - lo, lo - a, 1 + lo + (CAPP if lo >= mine else 0))
+
+    S.wait_ge(vs, places)
+    S.wait_ge(ss, cv)
+    V.wait_ge(vs, cu)
+    done = []
+    for k in range(2):
+        c = slice(128 * k, 128 * k + 128)
+        f = s(S.activation(T.first[:, c], T.zv[:, 0:1 + SL].indirect(T.offp[:, 8 * k:8 * k + 8]), F.Copy))
+        V.wait_ge(ss, f)
+        done.append(v(V.tensor_tensor(T.yt[:, c], T.zu[:, 0:1 + SL].indirect(T.offp[:, 16 + 8 * k:24 + 8 * k]), T.first[:, c], A.add)))
+    Y.wait_ge(vs, done[0])
+    Y.dma_start(T.y[:, 0:128], T.yt[:, 0:128]).then_inc(T.sem.st0, 16)
+    S.wait_ge(vs, done[1])
+    S.dma_start(T.y[:, 128:256], T.yt[:, 128:256]).then_inc(T.sem.st1, 16)
+    g.wait_ge(T.sem.sent, 2 * (N - 1))
+    Y.wait_ge(T.sem.st0, 16)
+    S.wait_ge(T.sem.st1, 16)

@@ -4,6 +4,7 @@ from concourse.mybir import dt, AluOpType, ActivationFunctionType
 N, CAPP, COLS, P = 8, 48, 256, 256
 SL = N * CAPP
 LW = SL // 16
+HR, HS, HL = N // 2, SL // 2, LW // 2
 LAND = (N - 1) * CAPP
 LEV = 7
 BY_S, BY_G = (1, 2), (3,)
@@ -67,7 +68,7 @@ SCRATCH = {
     "yt": ("sbuf", [128, P], "float32"),
     "ps": ("psum", [128, 4096], "float32"),
 }
-SEMAPHORES = ["vs", "ss", "ts", "gs", "lst", "lx", "la0", "la1", "la2", "la3", "luv", "lpl", "arr", "sent", "st0", "st1"]
+SEMAPHORES = ["vs", "ss", "ts", "gs", "lst", "lx", "la0", "la1", "la2", "la3", "luv", "lpl", "early", "late", "sent", "st0", "st1"]
 
 
 def half(h, k, bit):
@@ -87,6 +88,8 @@ def rank_program(g, core, T, topo):
     V, S, PE, Y = g.vector, g.scalar, g.tensor, g.sync
     A, F = AluOpType, ActivationFunctionType
     vs, ss, ts, gs = T.sem.vs, T.sem.ss, T.sem.ts, T.sem.gs
+    near = rank // HR
+    far = 1 - near
     n = {"v": 0, "s": 0, "t": 0, "g": 0}
 
     def v(i):
@@ -206,13 +209,22 @@ def rank_program(g, core, T, topo):
             last = v(V.tensor_tensor_scan(T.tab[:, TS * i + FK[k]:TS * i + FK[k] + w], m, rise, 0.0, A.mult, A.max))
         return last
 
-    def left(i, w):
+    def left(i, w, k):
         S.wait_ge(vs, w)
-        return s(S.activation(T.left[:, SL * i:SL * i + SL], T.tab[:, TS * i:TS * i + TW].indirect(T.offl[:, 0:LW]), F.Copy))
+        return s(S.activation(T.left[:, SL * i + HS * k:SL * i + HS * k + HS],
+                              T.tab[:, TS * i:TS * i + TW].indirect(T.offl[:, HL * k:HL * k + HL]), F.Copy))
 
-    def right(i, w):
+    def right(i, w, k):
         V.wait_ge(ss, w)
-        return v(V.tensor_tensor(T.pt[:, i:4 * SL:4], T.tab[:, TS * i:TS * i + TW].indirect(T.offr[:, 0:LW]), T.left[:, SL * i:SL * i + SL], A.max))
+        return v(V.tensor_tensor(T.pt[:, 4 * HS * k + i:4 * HS * (k + 1):4],
+                                 T.tab[:, TS * i:TS * i + TW].indirect(T.offr[:, HL * k:HL * k + HL]),
+                                 T.left[:, SL * i + HS * k:SL * i + HS * k + HS], A.max))
+
+    def pieces(k, w):
+        for i in range(4):
+            full = right(i, w[i], k)
+        V.wait_ge(vs, full)
+        return v(V.quantize_mx(T.qp[:, HS * k:HS * k + HS], T.sp[:, HS * k:HS * k + HS], T.pt[:, 4 * HS * k:4 * HS * (k + 1)]))
 
     V.wait_ge(T.sem.lx, 16)
     v(V.quantize_mx(T.qx[:], T.sx[:], T.xt[:]))
@@ -222,36 +234,43 @@ def rank_program(g, core, T, topo):
     r0 = result(0, z0)
     r1 = result(1, z1)
     V.wait_ge(vs, offs)
+    wf, wn = [0] * 4, [0] * 4
     w0 = tables(0, r0)
     r2 = result(2, product_a(2))
-    l0 = left(0, w0)
+    wf[0] = left(0, w0, far)
     w1 = tables(1, r1)
     r3 = result(3, product_a(3))
-    l1 = left(1, w1)
+    wf[1] = left(1, w1, far)
+    wn[0] = left(0, w0, near)
     w2 = tables(2, r2)
-    l2 = left(2, w2)
-    right(0, l0)
+    wf[2] = left(2, w2, far)
+    wn[1] = left(1, w1, near)
     w3 = tables(3, r3)
-    l3 = left(3, w3)
-    right(1, l1)
-    right(2, l2)
-    full = right(3, l3)
-    V.wait_ge(vs, full)
-    pieces = v(V.quantize_mx(T.qp[:], T.sp[:], T.pt[:]))
+    wf[3] = left(3, w3, far)
+    wn[2] = left(2, w2, near)
+    wn[3] = left(3, w3, near)
+    qf = pieces(far, wf)
+    qn = pieces(near, wn)
 
-    g.wait_ge(vs, pieces)
-    for src, dst, codes in (("qp", "lc", True), ("sp", "ls", False)):
-        tr = []
-        for i, r in enumerate([r for r in range(N) if r != rank]):
-            d = T.cores[r]
-            rid, pid = topo.addr(d, core)
-            at = CAPP * (rank if rank < r else rank - 1)
-            a, b = T[src][:, CAPP * r:CAPP * r + CAPP], T[dst][:, at:at + CAPP]
-            if codes:
-                a, b = a.bitcast(dt.uint8), b.bitcast(dt.uint8)
-            tr.append(RemoteDMATransfer(dst_ids=[DstId(rid=rid, pnc=pid)], dma_engine_mask=1 << topo.engines(core, d)[i],
-                                        remote_sem=T.sem.arr, src=a, dst=b))
-        g.remote_dma_fused(tr, local_sem=T.sem.sent)
+    def send(k, q, sem):
+        g.wait_ge(vs, q)
+        for src, dst, codes in (("qp", "lc", True), ("sp", "ls", False)):
+            tr = []
+            for i, r in enumerate([r for r in range(HR * k, HR * k + HR) if r != rank]):
+                d = T.cores[r]
+                rid, pid = topo.addr(d, core)
+                at = CAPP * (rank if rank < r else rank - 1)
+                a, b = T[src][:, CAPP * r:CAPP * r + CAPP], T[dst][:, at:at + CAPP]
+                if codes:
+                    a, b = a.bitcast(dt.uint8), b.bitcast(dt.uint8)
+                e = topo.engines(core, d)
+                e = e[2 * i:2 * i + 2] if codes or k == far else e[2 * i + 2:2 * i + 4]
+                tr.append(RemoteDMATransfer(dst_ids=[DstId(rid=rid, pnc=pid)], dma_engine_mask=(1 << e[0]) | (1 << e[1]),
+                                            remote_sem=sem, src=a, dst=b))
+            g.remote_dma_fused(tr, local_sem=T.sem.sent)
+
+    send(far, qf, T.sem.early)
+    send(near, qn, T.sem.late)
 
     V.wait_ge(T.sem.luv, 32)
     quv = v(V.quantize_mx(T.quv[:], T.suv[:], T.uvt[:]))
@@ -260,36 +279,30 @@ def rank_program(g, core, T, topo):
     V.wait_ge(T.sem.lpl, 256)
     places = v(V.tensor_scalar(T.offp[:], T.lp[:], 1, None, A.add))
 
-    def product(b, w, c0, codes, scales, a0):
-        return t(PE.matmul_mx(bank(b, w), T.quv[:, c0:c0 + 128], T.suv[:, c0:c0 + 128], codes[:, a0:a0 + w], scales[:, a0:a0 + w], True, True))
-
-    def copy_v(b, z, w, a, to):
-        S.wait_ge(ts, z)
-        return s(S.activation(T.zv[:, to:to + w], T.ps[:, 512 * b + a:512 * b + a + w], F.Copy))
-
-    def copy_u(b, z, w, a, to):
-        V.wait_ge(ts, z)
-        return v(V.tensor_copy(T.zu[:, to:to + w], T.ps[:, 512 * b + a:512 * b + a + w]))
-
-    own = min(CAPP * rank, SL - 128)
-    PE.wait_ge(vs, quv)
-    PE.wait_ge(ss, l3)
-    z = product(4, 128, 128, T.qp, T.sp, own)
-    copy_v(4, z, CAPP, CAPP * rank - own, 1 + CAPP * rank)
-    z = product(5, 128, 0, T.qp, T.sp, own)
-    copy_u(5, z, CAPP, CAPP * rank - own, 1 + CAPP * rank)
+    def products(bv, codes, scales, a, b, parts):
+        for bk, c0 in ((bv, 128), (bv + 1, 0)):
+            z = t(PE.matmul_mx(bank(bk, b - a), T.quv[:, c0:c0 + 128], T.suv[:, c0:c0 + 128], codes[:, a:b], scales[:, a:b], True, True))
+            for lo, hi, slot in parts:
+                src = T.ps[:, 512 * bk + lo - a:512 * bk + hi - a]
+                if c0:
+                    S.wait_ge(ts, z)
+                    cv = s(S.activation(T.zv[:, 1 + slot:1 + slot + hi - lo], src, F.Copy))
+                else:
+                    V.wait_ge(ts, z)
+                    cu = v(V.tensor_copy(T.zu[:, 1 + slot:1 + slot + hi - lo], src))
+        return cv, cu
 
     mine = CAPP * rank
-    cut = mine if 128 <= mine <= LAND - 128 else LAND // 2
-    PE.wait_ge(T.sem.arr, 2 * (N - 1))
-    for a, b, bv, bu in ((0, cut, 6, 7), (cut, LAND, 0, 1)):
-        parts = [(lo, hi) for lo, hi in ((a, min(b, mine)), (max(a, mine), b)) if lo < hi]
-        z = product(bv, b - a, 128, T.lc, T.ls, a)
-        for lo, hi in parts:
-            cv = copy_v(bv, z, hi - lo, lo - a, 1 + lo + (CAPP if lo >= mine else 0))
-        z = product(bu, b - a, 0, T.lc, T.ls, a)
-        for lo, hi in parts:
-            cu = copy_u(bu, z, hi - lo, lo - a, 1 + lo + (CAPP if lo >= mine else 0))
+    own = min(mine, SL - 128)
+    PE.wait_ge(vs, quv)
+    PE.wait_ge(ss, wn[3])
+    products(4, T.qp, T.sp, own, own + 128, [(mine, mine + CAPP, mine)])
+    PE.wait_ge(T.sem.early, 4 * HR)
+    f0 = HS - CAPP if far else 0
+    products(6, T.lc, T.ls, f0, f0 + HS, [(f0, f0 + HS, HS * far)])
+    PE.wait_ge(T.sem.late, 4 * (HR - 1))
+    n0, n1 = HS * near, HS * near + HS - CAPP
+    cv, cu = products(0, T.lc, T.ls, n0, n1, [p for p in ((n0, mine, n0), (mine, n1, mine + CAPP)) if p[0] < p[1]])
 
     S.wait_ge(vs, places)
     S.wait_ge(ss, cv)
@@ -304,6 +317,6 @@ def rank_program(g, core, T, topo):
     Y.dma_start(T.y[:, 0:128], T.yt[:, 0:128]).then_inc(T.sem.st0, 16)
     S.wait_ge(vs, done[1])
     S.dma_start(T.y[:, 128:256], T.yt[:, 128:256]).then_inc(T.sem.st1, 16)
-    g.wait_ge(T.sem.sent, 2 * (N - 1))
+    g.wait_ge(T.sem.sent, 4 * (N - 1))
     Y.wait_ge(T.sem.st0, 16)
     S.wait_ge(T.sem.st1, 16)

@@ -4,8 +4,9 @@ from concourse.mybir import dt, AluOpType, ActivationFunctionType
 N, CAPP, COLS, P = 8, 48, 256, 256
 SL = N * CAPP
 LW = SL // 16
-HR, HS, HL = N // 2, SL // 2, LW // 2
 LAND = (N - 1) * CAPP
+AT = (0, 4 * CAPP, 6 * CAPP, 8 * CAPP)
+RUN = 128
 LEV = 7
 BY_S, BY_G = (1, 2), (3,)
 PACKED = BY_S + BY_G
@@ -56,8 +57,12 @@ SCRATCH = {
     "pk": ("sbuf", [128, 4 * len(PACKED) * COLS], "bfloat16"),
     "left": ("sbuf", [128, 4 * SL], "bfloat16"),
     "pt": ("sbuf", [128, 4 * SL], "bfloat16"),
-    "qp": ("sbuf", [128, SL], "float8_e4m3fn_x4"),
-    "sp": ("sbuf", [128, SL], "uint8"),
+    "q0": ("sbuf", [128, 4 * CAPP], "float8_e4m3fn_x4"),
+    "s0": ("sbuf", [128, 4 * CAPP], "uint8"),
+    "q1": ("sbuf", [128, RUN], "float8_e4m3fn_x4"),
+    "s1": ("sbuf", [128, RUN], "uint8"),
+    "q2": ("sbuf", [128, RUN], "float8_e4m3fn_x4"),
+    "s2": ("sbuf", [128, RUN], "uint8"),
     "lc": ("sbuf", [128, LAND], "float8_e4m3fn_x4"),
     "ls": ("sbuf", [128, LAND], "uint8"),
     "lp": ("sbuf", [128, 32], "int32"),
@@ -68,7 +73,8 @@ SCRATCH = {
     "yt": ("sbuf", [128, P], "float32"),
     "ps": ("psum", [128, 4096], "float32"),
 }
-SEMAPHORES = ["vs", "ss", "ts", "gs", "lst", "lx", "la0", "la1", "la2", "la3", "luv", "lpl", "early", "late", "sent", "st0", "st1"]
+SEMAPHORES = ["vs", "ss", "ts", "gs", "lst", "lx", "la0", "la1", "la2", "la3", "luv", "lpl", "got0", "got1", "got2", "sent",
+              "st0", "st1"]
 
 
 def half(h, k, bit):
@@ -81,6 +87,11 @@ def falling(buf, a, w):
     return buf[:, a + w - 1:(a - 1 if a else None):-1]
 
 
+def groups(rank):
+    h, p = rank // 4, rank // 2
+    return 4 * (1 - h), 2 * (p ^ 1), 2 * p
+
+
 def rank_program(g, core, T, topo):
     rank = T.rank_of(core)
     if rank is None:
@@ -88,8 +99,7 @@ def rank_program(g, core, T, topo):
     V, S, PE, Y = g.vector, g.scalar, g.tensor, g.sync
     A, F = AluOpType, ActivationFunctionType
     vs, ss, ts, gs = T.sem.vs, T.sem.ss, T.sem.ts, T.sem.gs
-    near = rank // HR
-    far = 1 - near
+    group = groups(rank)
     n = {"v": 0, "s": 0, "t": 0, "g": 0}
 
     def v(i):
@@ -153,18 +163,6 @@ def rank_program(g, core, T, topo):
         s(S.activation(T.cb[:, 7 - j::8], T.tj[:, 8 * LW + 8 - j::8], F.Identity, bias=BK[j] - 1 + w + 129 * w, scale=-w))
         cands = s(S.activation(T.cf[:, 7 - j::8], T.tj[:, 8 * LW + 8 - j::8], F.Identity, bias=FK[j] - 1 - w + 129 * w, scale=-w))
 
-    def offsets():
-        V.wait_ge(ss, floors)
-        d = v(V.tensor_tensor(T.dif[:], T.tj[:, 8 * LW:16 * LW], T.tj[:, 0:8 * LW], A.is_gt))
-        V.wait_ge(ss, cands)
-        V.wait_ge(vs, d)
-        b = v(V.tensor_tensor_scan(T.pb[:], T.dif[:], T.cb[:], 0.0, A.mult, A.max))
-        f = v(V.tensor_tensor_scan(T.pq[:], T.dif[:], T.cf[:], 0.0, A.mult, A.max))
-        V.wait_ge(vs, b)
-        v(V.tensor_tensor(T.offl[:], T.pb[:, 7::8], T.lr[:, 0:LW], A.add))
-        V.wait_ge(vs, f)
-        return v(V.tensor_tensor(T.offr[:], T.pq[:, 7::8], T.lr[:, LW:2 * LW], A.add))
-
     def product_a(i):
         V.wait_ge(T.sem["la%d" % i], 16)
         c = slice(128 * i, 128 * i + 128)
@@ -178,10 +176,12 @@ def rank_program(g, core, T, topo):
     def result(i, z):
         S.wait_ge(ts, z)
         r = s(S.activation(T.tab[:, TS * i + 1:TS * i + 1 + COLS], bank(i, COLS), F.Relu, scale=0.05))
+        return r, s(S.activation(T["h%d" % i][:], bank(i, COLS), F.Relu, scale=0.05))
+
+    def pack(i, r):
         h = T["h%d" % i]
-        c = s(S.activation(h[:], bank(i, COLS), F.Relu, scale=0.05))
-        S.wait_ge(ss, c)
-        g.wait_ge(ss, c)
+        S.wait_ge(ss, r[1])
+        g.wait_ge(ss, r[1])
         ready = {}
         for k in PACKED:
             for bit in (0, 1):
@@ -190,87 +190,107 @@ def rank_program(g, core, T, topo):
                     ready[k] = (ss, s(S.activation(T.pk[:, a:a + 128], half(h, k, bit), F.Copy)))
                 else:
                     ready[k] = (gs, gp(g.affine_select(T.pk[:, a:a + 128], half(h, k, bit), [[0, 128]], A.is_equal, 0.0, 0, 0)))
-        return r, ready
+        return ready
 
-    def tables(i, r):
-        h, ready = r
-        V.wait_ge(ss, h)
+    def scans(i, k, fall, rise):
+        w = width(k)
+        m = T.mask[:, MK[k]:MK[k] + w]
+        v(V.tensor_tensor_scan(falling(T.tab, TS * i + BK[k], w), m, fall, 0.0, A.mult, A.max))
+        return v(V.tensor_tensor_scan(T.tab[:, TS * i + FK[k]:TS * i + FK[k] + w], m, rise, 0.0, A.mult, A.max))
+
+    def high(i, r):
+        V.wait_ge(ss, r[0])
         V.wait_ge(vs, consts)
         for k in range(LEV, 0, -1):
-            w, h0 = width(k), TS * i + 1
-            m = T.mask[:, MK[k]:MK[k] + w]
-            if k in PACKED:
-                V.wait_ge(*ready[k])
-                fall = falling(T.pk, packed(i, k, 0), 128)
-                rise = T.pk[:, packed(i, k, 1):packed(i, k, 1) + 128]
-            else:
-                fall, rise = falling(T.tab, h0, w), T.tab[:, h0 + COLS - w:h0 + COLS]
-            v(V.tensor_tensor_scan(falling(T.tab, TS * i + BK[k], w), m, fall, 0.0, A.mult, A.max))
-            last = v(V.tensor_tensor_scan(T.tab[:, TS * i + FK[k]:TS * i + FK[k] + w], m, rise, 0.0, A.mult, A.max))
+            if k not in PACKED:
+                w, h0 = width(k), TS * i + 1
+                scans(i, k, falling(T.tab, h0, w), T.tab[:, h0 + COLS - w:h0 + COLS])
+
+    def low(i, ready):
+        for k in PACKED:
+            V.wait_ge(*ready[k])
+            a, b = packed(i, k, 0), packed(i, k, 1)
+            last = scans(i, k, falling(T.pk, a, 128), T.pk[:, b:b + 128])
         return last
-
-    def left(i, w, k):
-        S.wait_ge(vs, w)
-        return s(S.activation(T.left[:, SL * i + HS * k:SL * i + HS * k + HS],
-                              T.tab[:, TS * i:TS * i + TW].indirect(T.offl[:, HL * k:HL * k + HL]), F.Copy))
-
-    def right(i, w, k):
-        V.wait_ge(ss, w)
-        return v(V.tensor_tensor(T.pt[:, 4 * HS * k + i:4 * HS * (k + 1):4],
-                                 T.tab[:, TS * i:TS * i + TW].indirect(T.offr[:, HL * k:HL * k + HL]),
-                                 T.left[:, SL * i + HS * k:SL * i + HS * k + HS], A.max))
-
-    def pieces(k, w):
-        for i in range(4):
-            full = right(i, w[i], k)
-        V.wait_ge(vs, full)
-        return v(V.quantize_mx(T.qp[:, HS * k:HS * k + HS], T.sp[:, HS * k:HS * k + HS], T.pt[:, 4 * HS * k:4 * HS * (k + 1)]))
 
     V.wait_ge(T.sem.lx, 16)
     v(V.quantize_mx(T.qx[:], T.sx[:], T.xt[:]))
+    V.wait_ge(ss, floors)
+    d = v(V.tensor_tensor(T.dif[:], T.tj[:, 8 * LW:16 * LW], T.tj[:, 0:8 * LW], A.is_gt))
     z0 = product_a(0)
-    offs = offsets()
+    V.wait_ge(ss, cands)
+    V.wait_ge(vs, d)
+    b = v(V.tensor_tensor_scan(T.pb[:], T.dif[:], T.cb[:], 0.0, A.mult, A.max))
+    f = v(V.tensor_tensor_scan(T.pq[:], T.dif[:], T.cf[:], 0.0, A.mult, A.max))
+    V.wait_ge(vs, b)
+    v(V.tensor_tensor(T.offl[:], T.pb[:, 7::8], T.lr[:, 0:LW], A.add))
+    V.wait_ge(vs, f)
+    offs = v(V.tensor_tensor(T.offr[:], T.pq[:, 7::8], T.lr[:, LW:2 * LW], A.add))
     z1 = product_a(1)
     r0 = result(0, z0)
     r1 = result(1, z1)
-    V.wait_ge(vs, offs)
-    wf, wn = [0] * 4, [0] * 4
-    w0 = tables(0, r0)
+    p0 = pack(0, r0)
+    p1 = pack(1, r1)
+    high(0, r0)
     r2 = result(2, product_a(2))
-    wf[0] = left(0, w0, far)
-    w1 = tables(1, r1)
+    p2 = pack(2, r2)
+    high(1, r1)
+    w0 = low(0, p0)
     r3 = result(3, product_a(3))
-    wf[1] = left(1, w1, far)
-    wn[0] = left(0, w0, near)
-    w2 = tables(2, r2)
-    wf[2] = left(2, w2, far)
-    wn[1] = left(1, w1, near)
-    w3 = tables(3, r3)
-    wf[3] = left(3, w3, far)
-    wn[2] = left(2, w2, near)
-    wn[3] = left(3, w3, near)
-    qf = pieces(far, wf)
-    qn = pieces(near, wn)
+    p3 = pack(3, r3)
+    high(2, r2)
+    w1 = low(1, p1)
+    high(3, r3)
+    w2 = low(2, p2)
+    w3 = low(3, p3)
 
-    def send(k, q, sem):
+    def left(j):
+        k, w, o = AT[j], AT[j + 1] - AT[j], CAPP * group[j] // 16
+        done = []
+        for i, c in enumerate((w0, w1, w2, w3)):
+            S.wait_ge(vs, max(c, offs))
+            done.append(s(S.activation(T.left[:, SL * i + k:SL * i + k + w],
+                                       T.tab[:, TS * i:TS * i + TW].indirect(T.offl[:, o:o + w // 16]), F.Copy)))
+        return done
+
+    def right(j, lefts):
+        k, w, o = AT[j], AT[j + 1] - AT[j], CAPP * group[j] // 16
+        V.wait_ge(vs, offs)
+        for i in range(4):
+            V.wait_ge(ss, lefts[i])
+            full = v(V.tensor_tensor(T.pt[:, 4 * k + i:4 * (k + w):4],
+                                     T.tab[:, TS * i:TS * i + TW].indirect(T.offr[:, o:o + w // 16]),
+                                     T.left[:, SL * i + k:SL * i + k + w], A.max))
+        V.wait_ge(vs, full)
+        w = max(w, RUN)
+        return v(V.quantize_mx(T["q%d" % j][:], T["s%d" % j][:], T.pt[:, 4 * (AT[j + 1] - w):4 * AT[j + 1]]))
+
+    def send(j, q):
+        to = [r for r in range(group[j], group[j] + (AT[j + 1] - AT[j]) // CAPP) if r != rank]
+        first = RUN - 2 * CAPP if j else 0
         g.wait_ge(vs, q)
-        for src, dst, codes in (("qp", "lc", True), ("sp", "ls", False)):
+        for src, dst, codes in (("q%d" % j, "lc", True), ("s%d" % j, "ls", False)):
             tr = []
-            for i, r in enumerate([r for r in range(HR * k, HR * k + HR) if r != rank]):
+            for i, r in enumerate(to):
                 d = T.cores[r]
                 rid, pid = topo.addr(d, core)
-                at = CAPP * (rank if rank < r else rank - 1)
-                a, b = T[src][:, CAPP * r:CAPP * r + CAPP], T[dst][:, at:at + CAPP]
+                at = AT[j] + CAPP * (rank - groups(r)[j] if j < 2 else 0)
+                c = first + CAPP * (r - group[j])
+                a, b = T[src][:, c:c + CAPP], T[dst][:, at:at + CAPP]
                 if codes:
                     a, b = a.bitcast(dt.uint8), b.bitcast(dt.uint8)
                 e = topo.engines(core, d)
-                e = e[2 * i:2 * i + 2] if codes or k == far else e[2 * i + 2:2 * i + 4]
-                tr.append(RemoteDMATransfer(dst_ids=[DstId(rid=rid, pnc=pid)], dma_engine_mask=(1 << e[0]) | (1 << e[1]),
-                                            remote_sem=sem, src=a, dst=b))
+                w = len(e) // len(to)
+                tr.append(RemoteDMATransfer(dst_ids=[DstId(rid=rid, pnc=pid)], dma_engine_mask=sum(1 << x for x in e[w * i:w * i + w]),
+                                            remote_sem=T.sem["got%d" % j], src=a, dst=b))
             g.remote_dma_fused(tr, local_sem=T.sem.sent)
+        return 2 * w * len(to)
 
-    send(far, qf, T.sem.early)
-    send(near, qn, T.sem.late)
+    lefts = [left(j) for j in range(3)]
+    sent = 0
+    for j in range(3):
+        last = right(j, lefts[j])
+        sent = sent + send(j, last)
 
     V.wait_ge(T.sem.luv, 32)
     quv = v(V.quantize_mx(T.quv[:], T.suv[:], T.uvt[:]))
@@ -279,30 +299,27 @@ def rank_program(g, core, T, topo):
     V.wait_ge(T.sem.lpl, 256)
     places = v(V.tensor_scalar(T.offp[:], T.lp[:], 1, None, A.add))
 
-    def products(bv, codes, scales, a, b, parts):
+    def products(bv, codes, scales, a, b, lo, hi, slot):
         for bk, c0 in ((bv, 128), (bv + 1, 0)):
             z = t(PE.matmul_mx(bank(bk, b - a), T.quv[:, c0:c0 + 128], T.suv[:, c0:c0 + 128], codes[:, a:b], scales[:, a:b], True, True))
-            for lo, hi, slot in parts:
-                src = T.ps[:, 512 * bk + lo - a:512 * bk + hi - a]
-                if c0:
-                    S.wait_ge(ts, z)
-                    cv = s(S.activation(T.zv[:, 1 + slot:1 + slot + hi - lo], src, F.Copy))
-                else:
-                    V.wait_ge(ts, z)
-                    cu = v(V.tensor_copy(T.zu[:, 1 + slot:1 + slot + hi - lo], src))
+            src = T.ps[:, 512 * bk + lo - a:512 * bk + hi - a]
+            if c0:
+                S.wait_ge(ts, z)
+                cv = s(S.activation(T.zv[:, 1 + slot:1 + slot + hi - lo], src, F.Copy))
+            else:
+                V.wait_ge(ts, z)
+                cu = v(V.tensor_copy(T.zu[:, 1 + slot:1 + slot + hi - lo], src))
         return cv, cu
 
-    mine = CAPP * rank
-    own = min(mine, SL - 128)
+    own = RUN - 2 * CAPP + CAPP * (rank - group[2])
     PE.wait_ge(vs, quv)
-    PE.wait_ge(ss, wn[3])
-    products(4, T.qp, T.sp, own, own + 128, [(mine, mine + CAPP, mine)])
-    PE.wait_ge(T.sem.early, 4 * HR)
-    f0 = HS - CAPP if far else 0
-    products(6, T.lc, T.ls, f0, f0 + HS, [(f0, f0 + HS, HS * far)])
-    PE.wait_ge(T.sem.late, 4 * (HR - 1))
-    n0, n1 = HS * near, HS * near + HS - CAPP
-    cv, cu = products(0, T.lc, T.ls, n0, n1, [p for p in ((n0, mine, n0), (mine, n1, mine + CAPP)) if p[0] < p[1]])
+    PE.wait_ge(ss, lefts[2][3])
+    products(4, T.q2, T.s2, 0, RUN, own, own + CAPP, CAPP * rank)
+    for j, bk in ((0, 6), (1, 0), (2, 2)):
+        end = AT[j + 1] if j < 2 else LAND
+        PE.wait_ge(T.sem["got%d" % j], 16)
+        slot = CAPP * (group[j] if j < 2 else rank ^ 1)
+        cv, cu = products(bk, T.lc, T.ls, end - max(end - AT[j], RUN), end, AT[j], end, slot)
 
     S.wait_ge(vs, places)
     S.wait_ge(ss, cv)
@@ -317,6 +334,6 @@ def rank_program(g, core, T, topo):
     Y.dma_start(T.y[:, 0:128], T.yt[:, 0:128]).then_inc(T.sem.st0, 16)
     S.wait_ge(vs, done[1])
     S.dma_start(T.y[:, 128:256], T.yt[:, 128:256]).then_inc(T.sem.st1, 16)
-    g.wait_ge(T.sem.sent, 4 * (N - 1))
+    g.wait_ge(T.sem.sent, sent)
     Y.wait_ge(T.sem.st0, 16)
     S.wait_ge(T.sem.st1, 16)

from concourse.bass import DstId, RemoteDMATransfer
from concourse.mybir import dt, AluOpType, ActivationFunctionType

N, CAPP, COLS, P = 8, 48, 256, 256
SL = N * CAPP
LW = SL // 16
LAND = (N - 1) * CAPP
AT = (0, 4 * CAPP, 6 * CAPP, 8 * CAPP)
RUN = 128
LEV = 7
BY_S, BY_G = (1, 2), (3,)
PACKED = BY_S + BY_G
ZW = 392


def width(k):
    return COLS // 2 if k in PACKED else COLS - (1 << k)


def layout():
    b, f, m, at, am = {}, {}, {}, 2 + COLS, 0
    for k in range(1, LEV + 1):
        b[k], f[k], m[k] = at, at + width(k), am
        at, am = at + 2 * width(k), am + width(k)
    return b, f, m, at, am


BK, FK, MK, TW, MW = layout()
TS = (TW + 15) // 16 * 16

SCRATCH = {
    "lol": ("sbuf", [128, 2 * LW], "int32"),
    "lr": ("sbuf", [128, 2 * LW], "float32"),
    "tj": ("sbuf", [128, 16 * LW], "bfloat16"),
    "dif": ("sbuf", [128, 8 * LW], "float32"),
    "cb": ("sbuf", [128, 8 * LW], "float32"),
    "cf": ("sbuf", [128, 8 * LW], "float32"),
    "pb": ("sbuf", [128, 8 * LW], "float32"),
    "pq": ("sbuf", [128, 8 * LW], "float32"),
    "offl": ("sbuf", [128, LW], "uint16"),
    "offr": ("sbuf", [128, LW], "uint16"),
    "xt": ("sbuf", [128, 1024], "bfloat16"),
    "at": ("sbuf", [128, 2048], "bfloat16"),
    "uvt": ("sbuf", [128, 1024], "bfloat16"),
    "qx": ("sbuf", [128, 256], "float8_e4m3fn_x4"),
    "sx": ("sbuf", [128, 256], "uint8"),
    "qa": ("sbuf", [128, 512], "float8_e4m3fn_x4"),
    "sa": ("sbuf", [128, 512], "uint8"),
    "quv": ("sbuf", [128, 256], "float8_e4m3fn_x4"),
    "suv": ("sbuf", [128, 256], "uint8"),
    "h0": ("sbuf", [128, 4, 4, 4, 4], "bfloat16"),
    "h1": ("sbuf", [128, 4, 4, 4, 4], "bfloat16"),
    "h2": ("sbuf", [128, 4, 4, 4, 4], "bfloat16"),
    "h3": ("sbuf", [128, 4, 4, 4, 4], "bfloat16"),
    "tab": ("sbuf", [128, 4 * TS], "bfloat16"),
    "mask": ("sbuf", [128, MW], "bfloat16"),
    "pk": ("sbuf", [128, 4 * len(PACKED) * COLS], "bfloat16"),
    "left": ("sbuf", [128, 4 * SL], "bfloat16"),
    "pt": ("sbuf", [128, 4 * SL], "bfloat16"),
    "q0": ("sbuf", [128, 4 * CAPP], "float8_e4m3fn_x4"),
    "s0": ("sbuf", [128, 4 * CAPP], "uint8"),
    "q1": ("sbuf", [128, RUN], "float8_e4m3fn_x4"),
    "s1": ("sbuf", [128, RUN], "uint8"),
    "q2": ("sbuf", [128, RUN], "float8_e4m3fn_x4"),
    "s2": ("sbuf", [128, RUN], "uint8"),
    "lc": ("sbuf", [128, LAND], "float8_e4m3fn_x4"),
    "ls": ("sbuf", [128, LAND], "uint8"),
    "lp": ("sbuf", [128, 32], "int32"),
    "offp": ("sbuf", [128, 32], "uint16"),
    "zv": ("sbuf", [128, ZW], "float32"),
    "zu": ("sbuf", [128, ZW], "float32"),
    "first": ("sbuf", [128, P], "float32"),
    "yt": ("sbuf", [128, P], "float32"),
    "ps": ("psum", [128, 4096], "float32"),
}
SEMAPHORES = ["vs", "ss", "ts", "gs", "lst", "lx", "la0", "la1", "la2", "la3", "luv", "lpl", "got0", "got1", "got2", "sent",
              "st0", "st1"]


def half(h, k, bit):
    ix = [slice(None)] * 5
    ix[4 - k // 2] = slice(2 * bit, 2 * bit + 2) if k % 2 else slice(bit, None, 2)
    return h[tuple(ix)]


def falling(buf, a, w):
    return buf[:, a + w - 1:(a - 1 if a else None):-1]


def groups(rank):
    h, p = rank // 4, rank // 2
    return 4 * (1 - h), 2 * (p ^ 1), 2 * p


def rank_program(g, core, T, topo):
    rank = T.rank_of(core)
    if rank is None:
        return
    V, S, PE, Y = g.vector, g.scalar, g.tensor, g.sync
    A, F = AluOpType, ActivationFunctionType
    vs, ss, ts, gs = T.sem.vs, T.sem.ss, T.sem.ts, T.sem.gs
    group = groups(rank)
    n = {"v": 0, "s": 0, "t": 0, "g": 0}

    def v(i):
        n["v"] += 1
        i.then_inc(vs, 1)
        return n["v"]

    def s(i):
        n["s"] += 1
        i.then_inc(ss, 1)
        return n["s"]

    def t(i):
        n["t"] += 1
        i.then_inc(ts, 1)
        return n["t"]

    def gp(i):
        n["g"] += 1
        i.then_inc(gs, 1)
        return n["g"]

    def bank(b, w):
        return T.ps[:, 512 * b:512 * b + w]

    S.dma_start(T.lol[:, 0:LW], T.lo[:]).then_inc(T.sem.lst, 16)
    S.dma_start(T.lol[:, LW:2 * LW], T.ln[:]).then_inc(T.sem.lst, 16)
    Y.dma_start(T.xt[:], T.x[:]).then_inc(T.sem.lx, 16)
    for i in range(4):
        Y.dma_start(T["at"][:, 512 * i:512 * i + 512], T.a[:, 512 * i:512 * i + 512]).then_inc(T.sem["la%d" % i], 16)
    Y.dma_start(T.uvt[:, 0:512], T.u[:]).then_inc(T.sem.luv, 16)
    Y.dma_start(T.uvt[:, 512:1024], T.v[:]).then_inc(T.sem.luv, 16)
    for k in range(8):
        Y.dma_start(T.lp[16 * k:16 * k + 16, 0:16], T.pf[:]).then_inc(T.sem.lpl, 16)
        Y.dma_start(T.lp[16 * k:16 * k + 16, 16:32], T.pg[:]).then_inc(T.sem.lpl, 16)

    ones = v(V.memset(T.mask[:], 1.0))
    v(V.memset(T.tj[:, 0::8], 0.0))
    v(V.memset(T.cb[:, 7::8], 0.0))
    v(V.memset(T.cf[:, 7::8], 0.0))
    v(V.memset(T.tab[:, 0::TS], 0.0))
    v(V.memset(T.tab[:, 1 + COLS::TS], 0.0))
    for k in range(1, LEV + 1):
        if k not in PACKED:
            v(V.memset(T.cb[:, 7 - k::8], BK[k] - 1.0))
            v(V.memset(T.cf[:, 7 - k::8], FK[k] - (1 << k) - 1.0))

    V.wait_ge(T.sem.lst, 32)
    v(V.tensor_scalar(T.lr[:, 0:LW], T.lol[:, 0:LW], 1, None, A.add))
    lists = v(V.tensor_tensor(T.lr[:, LW:2 * LW], T.lol[:, 0:LW], T.lol[:, LW:2 * LW], A.add))
    V.wait_ge(vs, ones)
    for k in range(1, LEV + 1):
        consts = v(V.memset(T.mask[:, MK[k]:MK[k] + width(k):1 << k], 0.0))

    S.wait_ge(vs, lists)
    for j in range(LEV, 0, -1):
        floors = s(S.activation(T.tj[:, 8 - j::8], T.lr[:], F.Identity, bias=128.5 - 2.0 ** -(j + 1), scale=2.0 ** -j))
    S.wait_ge(ss, floors)
    for j in PACKED:
        w = 2.0 ** (j - 1)
        s(S.activation(T.cb[:, 7 - j::8], T.tj[:, 8 * LW + 8 - j::8], F.Identity, bias=BK[j] - 1 + w + 129 * w, scale=-w))
        cands = s(S.activation(T.cf[:, 7 - j::8], T.tj[:, 8 * LW + 8 - j::8], F.Identity, bias=FK[j] - 1 - w + 129 * w, scale=-w))

    def product_a(i):
        V.wait_ge(T.sem["la%d" % i], 16)
        c = slice(128 * i, 128 * i + 128)
        q = v(V.quantize_mx(T.qa[:, c], T.sa[:, c], T["at"][:, 512 * i:512 * i + 512]))
        PE.wait_ge(vs, q)
        return t(PE.matmul_mx(bank(i, COLS), T.qa[:, c], T.sa[:, c], T.qx[:], T.sx[:], True, True))

    def packed(i, k, bit):
        return COLS * (len(PACKED) * i + PACKED.index(k)) + 128 * bit

    def result(i, z):
        S.wait_ge(ts, z)
        r = s(S.activation(T.tab[:, TS * i + 1:TS * i + 1 + COLS], bank(i, COLS), F.Relu, scale=0.05))
        return r, s(S.activation(T["h%d" % i][:], bank(i, COLS), F.Relu, scale=0.05))

    def pack(i, r):
        h = T["h%d" % i]
        S.wait_ge(ss, r[1])
        g.wait_ge(ss, r[1])
        ready = {}
        for k in PACKED:
            for bit in (0, 1):
                a = packed(i, k, bit)
                if k in BY_S:
                    ready[k] = (ss, s(S.activation(T.pk[:, a:a + 128], half(h, k, bit), F.Copy)))
                else:
                    ready[k] = (gs, gp(g.affine_select(T.pk[:, a:a + 128], half(h, k, bit), [[0, 128]], A.is_equal, 0.0, 0, 0)))
        return ready

    def scans(i, k, fall, rise):
        w = width(k)
        m = T.mask[:, MK[k]:MK[k] + w]
        v(V.tensor_tensor_scan(falling(T.tab, TS * i + BK[k], w), m, fall, 0.0, A.mult, A.max))
        return v(V.tensor_tensor_scan(T.tab[:, TS * i + FK[k]:TS * i + FK[k] + w], m, rise, 0.0, A.mult, A.max))

    def high(i, r):
        V.wait_ge(ss, r[0])
        V.wait_ge(vs, consts)
        for k in range(LEV, 0, -1):
            if k not in PACKED:
                w, h0 = width(k), TS * i + 1
                scans(i, k, falling(T.tab, h0, w), T.tab[:, h0 + COLS - w:h0 + COLS])

    def low(i, ready):
        for k in PACKED:
            V.wait_ge(*ready[k])
            a, b = packed(i, k, 0), packed(i, k, 1)
            last = scans(i, k, falling(T.pk, a, 128), T.pk[:, b:b + 128])
        return last

    V.wait_ge(T.sem.lx, 16)
    v(V.quantize_mx(T.qx[:], T.sx[:], T.xt[:]))
    V.wait_ge(ss, floors)
    d = v(V.tensor_tensor(T.dif[:], T.tj[:, 8 * LW:16 * LW], T.tj[:, 0:8 * LW], A.is_gt))
    z0 = product_a(0)
    V.wait_ge(ss, cands)
    V.wait_ge(vs, d)
    b = v(V.tensor_tensor_scan(T.pb[:], T.dif[:], T.cb[:], 0.0, A.mult, A.max))
    f = v(V.tensor_tensor_scan(T.pq[:], T.dif[:], T.cf[:], 0.0, A.mult, A.max))
    V.wait_ge(vs, b)
    v(V.tensor_tensor(T.offl[:], T.pb[:, 7::8], T.lr[:, 0:LW], A.add))
    V.wait_ge(vs, f)
    offs = v(V.tensor_tensor(T.offr[:], T.pq[:, 7::8], T.lr[:, LW:2 * LW], A.add))
    z1 = product_a(1)
    r0 = result(0, z0)
    r1 = result(1, z1)
    p0 = pack(0, r0)
    p1 = pack(1, r1)
    high(0, r0)
    r2 = result(2, product_a(2))
    p2 = pack(2, r2)
    high(1, r1)
    w0 = low(0, p0)
    r3 = result(3, product_a(3))
    p3 = pack(3, r3)
    high(2, r2)
    w1 = low(1, p1)
    high(3, r3)
    w2 = low(2, p2)
    w3 = low(3, p3)

    def left(j):
        k, w, o = AT[j], AT[j + 1] - AT[j], CAPP * group[j] // 16
        done = []
        for i, c in enumerate((w0, w1, w2, w3)):
            S.wait_ge(vs, max(c, offs))
            done.append(s(S.activation(T.left[:, SL * i + k:SL * i + k + w],
                                       T.tab[:, TS * i:TS * i + TW].indirect(T.offl[:, o:o + w // 16]), F.Copy)))
        return done

    def right(j, lefts):
        k, w, o = AT[j], AT[j + 1] - AT[j], CAPP * group[j] // 16
        V.wait_ge(vs, offs)
        for i in range(4):
            V.wait_ge(ss, lefts[i])
            full = v(V.tensor_tensor(T.pt[:, 4 * k + i:4 * (k + w):4],
                                     T.tab[:, TS * i:TS * i + TW].indirect(T.offr[:, o:o + w // 16]),
                                     T.left[:, SL * i + k:SL * i + k + w], A.max))
        V.wait_ge(vs, full)
        w = max(w, RUN)
        return v(V.quantize_mx(T["q%d" % j][:], T["s%d" % j][:], T.pt[:, 4 * (AT[j + 1] - w):4 * AT[j + 1]]))

    def send(j, q):
        to = [r for r in range(group[j], group[j] + (AT[j + 1] - AT[j]) // CAPP) if r != rank]
        first = RUN - 2 * CAPP if j else 0
        g.wait_ge(vs, q)
        for src, dst, codes in (("q%d" % j, "lc", True), ("s%d" % j, "ls", False)):
            tr = []
            for i, r in enumerate(to):
                d = T.cores[r]
                rid, pid = topo.addr(d, core)
                at = AT[j] + CAPP * (rank - groups(r)[j] if j < 2 else 0)
                c = first + CAPP * (r - group[j])
                a, b = T[src][:, c:c + CAPP], T[dst][:, at:at + CAPP]
                if codes:
                    a, b = a.bitcast(dt.uint8), b.bitcast(dt.uint8)
                e = topo.engines(core, d)
                w = len(e) // len(to)
                tr.append(RemoteDMATransfer(dst_ids=[DstId(rid=rid, pnc=pid)], dma_engine_mask=sum(1 << x for x in e[w * i:w * i + w]),
                                            remote_sem=T.sem["got%d" % j], src=a, dst=b))
            g.remote_dma_fused(tr, local_sem=T.sem.sent)
        return 2 * w * len(to)

    lefts = [left(j) for j in range(3)]
    sent = 0
    for j in range(3):
        last = right(j, lefts[j])
        sent = sent + send(j, last)

    V.wait_ge(T.sem.luv, 32)
    quv = v(V.quantize_mx(T.quv[:], T.suv[:], T.uvt[:]))
    v(V.memset(T.zv[:, 0:1], 0.0))
    v(V.memset(T.zu[:, 0:1], 0.0))
    V.wait_ge(T.sem.lpl, 256)
    places = v(V.tensor_scalar(T.offp[:], T.lp[:], 1, None, A.add))

    def products(bv, codes, scales, a, b, lo, hi, slot):
        for bk, c0 in ((bv, 128), (bv + 1, 0)):
            z = t(PE.matmul_mx(bank(bk, b - a), T.quv[:, c0:c0 + 128], T.suv[:, c0:c0 + 128], codes[:, a:b], scales[:, a:b], True, True))
            src = T.ps[:, 512 * bk + lo - a:512 * bk + hi - a]
            if c0:
                S.wait_ge(ts, z)
                cv = s(S.activation(T.zv[:, 1 + slot:1 + slot + hi - lo], src, F.Copy))
            else:
                V.wait_ge(ts, z)
                cu = v(V.tensor_copy(T.zu[:, 1 + slot:1 + slot + hi - lo], src))
        return cv, cu

    own = RUN - 2 * CAPP + CAPP * (rank - group[2])
    PE.wait_ge(vs, quv)
    PE.wait_ge(ss, lefts[2][3])
    products(4, T.q2, T.s2, 0, RUN, own, own + CAPP, CAPP * rank)
    for j, bk in ((0, 6), (1, 0), (2, 2)):
        end = AT[j + 1] if j < 2 else LAND
        PE.wait_ge(T.sem["got%d" % j], 16)
        slot = CAPP * (group[j] if j < 2 else rank ^ 1)
        cv, cu = products(bk, T.lc, T.ls, end - max(end - AT[j], RUN), end, AT[j], end, slot)

    S.wait_ge(vs, places)
    S.wait_ge(ss, cv)
    V.wait_ge(vs, cu)
    done = []
    for k in range(2):
        c = slice(128 * k, 128 * k + 128)
        f = s(S.activation(T.first[:, c], T.zv[:, 0:1 + SL].indirect(T.offp[:, 8 * k:8 * k + 8]), F.Copy))
        V.wait_ge(ss, f)
        done.append(v(V.tensor_tensor(T.yt[:, c], T.zu[:, 0:1 + SL].indirect(T.offp[:, 16 + 8 * k:24 + 8 * k]), T.first[:, c], A.add)))
    Y.wait_ge(vs, done[0])
    Y.dma_start(T.y[:, 0:128], T.yt[:, 0:128]).then_inc(T.sem.st0, 16)
    S.wait_ge(vs, done[1])
    S.dma_start(T.y[:, 128:256], T.yt[:, 128:256]).then_inc(T.sem.st1, 16)
    g.wait_ge(T.sem.sent, sent)
    Y.wait_ge(T.sem.st0, 16)
    S.wait_ge(T.sem.st1, 16)
